import numpy as np
import ml_dtypes


def mxq(x, axis, fmt="e4m3"):
    dtype, down = {"e4m3": (ml_dtypes.float8_e4m3fn, 7), "e5m2": (ml_dtypes.float8_e5m2, 14)}[fmt]
    v = np.moveaxis(np.asarray(x, np.float32).astype(ml_dtypes.bfloat16).astype(np.float64), axis, -1)
    blocks = v.reshape(v.shape[:-1] + (-1, 32))
    amax = np.abs(blocks).max(-1, keepdims=True)
    byte = np.maximum(np.where(amax > 0, np.frexp(amax)[1] - 1 + 127, 0) - down, 1)
    scale = np.exp2(byte - 127.0)
    codes = (blocks / scale).astype(np.float32).astype(dtype).astype(np.float64)
    return np.moveaxis((codes * scale).reshape(v.shape), -1, axis)


WIDE = False


def mx_kscale(k):
    if not WIDE:
        return np.ones(k)
    levels = np.array([10, -10, 5, -5, 0])
    if k % 512:
        return np.exp2(np.random.permutation(np.resize(levels, k // 32))).repeat(32)
    a = np.empty((k // 512, 16))
    for p in range(k // 512):
        a[p, :8] = np.random.permutation(np.resize(levels, 8))
        for g in range(8):
            far = levels[np.abs(levels - a[p, g]) >= 10]
            a[p, g + 8] = far[np.random.randint(len(far))]
    return np.exp2(a.ravel()).repeat(32)


def f64(x):
    return np.asarray(x).astype(np.float64)


def striped(idx):
    return np.tile(np.asarray(idx).reshape(-1, 16).T, (8, 1)).astype(np.uint16)


def unstriped(offs):
    return offs[:16].T.reshape(-1).astype(np.int64)


E2M1 = np.array([0.0, 0.5, 1.0, 1.5, 2.0, 3.0, 4.0, 6.0, -0.0, -0.5, -1.0, -1.5, -2.0, -3.0, -4.0, -6.0])


def pack_weight(w, fmt):
    k, n = w.shape
    w = f64(np.asarray(w, np.float32).astype(ml_dtypes.bfloat16)).reshape(k // 32, 32, n)
    amax = np.abs(w).max(1)
    if fmt == "e4m3":
        byte = np.frexp(amax)[1] - 1 + 127 - 7
    else:
        mant, ex = np.frexp(amax / 6.0)
        byte = np.where(mant > 0.5, ex, ex - 1) + 127
    byte = np.clip(np.where(amax > 0, byte, 1), 1, 254)
    scaled = (w * np.exp2(127.0 - byte)[:, None, :]).reshape(k, n).astype(np.float32)
    by_word = np.ascontiguousarray(scaled.reshape(k // 512, 128, 4, n).transpose(0, 1, 3, 2))
    if fmt == "e4m3":
        words = by_word.astype(ml_dtypes.float8_e4m3fn).view(np.uint8)
    else:
        c = by_word.astype(ml_dtypes.float4_e2m1fn).view(np.uint8) & 0xF
        words = (c[..., 0::2] | (c[..., 1::2] << 4)).reshape(k // 512, 128, 2 * n)
    return np.ascontiguousarray(words), np.ascontiguousarray(byte.astype(np.uint8).reshape(k // 512, 16, n))


def unpack_weight(words, scales, fmt):
    g, _, n = scales.shape
    words = np.ascontiguousarray(words).reshape(g, 128, n, -1)
    if fmt == "e4m3":
        vals = words.view(ml_dtypes.float8_e4m3fn).astype(np.float64)
    else:
        nib = np.empty((g, 128, n, 4), np.uint8)
        nib[..., 0::2] = words & 0xF
        nib[..., 1::2] = words >> 4
        vals = E2M1[nib]
    vals = vals * np.repeat(np.exp2(scales.astype(np.float64) - 127.0), 8, axis=1)[..., None]
    return vals.transpose(0, 1, 3, 2).reshape(g * 512, n)


D, E, T, I, U, Q = 512, 512, 1024, 512, 2048, 128


def setup_inputs():
    n = np.random.standard_normal
    idx = np.random.permutation(T)[:I]
    idx2 = np.random.permutation(U)[:I]
    fd = mx_kscale(D)
    fe = mx_kscale(E)
    cvalsp = pack_weight(n((E, T)) / fe[:, None], "e2m1")
    return {
        "query": (n((D, Q)) * 0.6 / np.sqrt(D) * fd[:, None]).astype(np.float32),
        "keys": (n((D, T)) / fd[:, None]).astype(np.float32),
        "gout": (n((E, Q)) * 1 / np.sqrt(E) * fe[:, None]).astype(np.float32),
        "cvals_words": cvalsp[0],
        "cvals_scales": cvalsp[1],
        "corr": (n((E, U)) / fe[:, None]).astype(np.float32),
        "us": (np.random.uniform(0.5, 2.0, (1, I))).astype(np.float32),
        "old": (0.5 * n((Q, T))).astype(np.float32),
        "offs": striped(idx),
        "offs2": striped(idx2),
    }


def reference(query, keys, gout, cvals_words, cvals_scales, corr, us, old, offs, offs2):
    idx = unstriped(offs)
    idx2 = unstriped(offs2)
    cvalsu = unpack_weight(cvals_words, cvals_scales, "e2m1")
    queryq = mxq(f64(query), 0, "e4m3")
    keysq = mxq(f64(keys), 0, "e4m3")
    a = queryq.T @ keysq
    m1 = np.max(a, axis=1, keepdims=True)
    p = np.exp(a - m1)
    z = np.sum(p, axis=1, keepdims=True)
    px = np.exp(a[:, idx] - m1)
    goutq = mxq(f64(gout), 0, "e4m3")
    c0 = goutq.T @ cvalsu
    corridx2q = mxq(f64(corr)[:, idx2], 0, "e4m3")
    c1 = goutq.T @ corridx2q
    dpx = 1.0 / z * c1 * f64(us)
    dz = (np.sum(p * c0, axis=1, keepdims=True) + np.sum(px * f64(us) * c1, axis=1, keepdims=True)) / np.square(z) * (-1.0)
    dp = 1.0 / z * c0 + dz
    e1 = dpx * px
    s1 = np.zeros((Q, T))
    s1[:, idx] = e1
    da = dp * p + s1
    y = da * 1024.0 + f64(old)
    return y

@@ -1,0 +1,201 @@
+from contextlib import ExitStack
+
+import concourse.mybir as mybir
+from concourse.masks import make_identity
+
+D, E, T, I, U, Q = 512, 512, 1024, 512, 2048, 128
+FLOPS = 2 * Q * (D * T + E * T + E * I)
+
+F32 = mybir.dt.float32
+BF16 = mybir.dt.bfloat16
+I32 = mybir.dt.int32
+U32 = mybir.dt.uint32
+U16 = mybir.dt.uint16
+U8 = mybir.dt.uint8
+FP8X4 = mybir.dt.float8_e4m3fn_x4
+FP4X4 = mybir.dt.float4_e2m1fn_x4
+ALU = mybir.AluOpType
+ACT = mybir.ActivationFunctionType
+AXIS = mybir.AxisListType
+
+P = 128
+PACK = 4
+BANK = 512
+KEY_CHUNK = 256
+KEY_VECTOR = 160
+HALF = 256
+STORE = 256
+GAIN = 1024.0
+
+
+def weave_views(grouped, raw, lo, hi):
+    dst = grouped[:, lo:hi, :].rearrange("p (c i) t -> p c t i", i=4)
+    src = raw[:, :, lo:hi].rearrange("p t (c i) -> p c t i", i=4)
+    return dst, src
+
+
+def tile_attend_bvaluepatch_kernel(tc, query, keys, gout, cvals_words, cvals_scales, corr, us, old, offs, offs2, out):
+    nc = tc.nc
+    with ExitStack() as ctx:
+        sb = ctx.enter_context(tc.tile_pool(name="sb", bufs=1))
+        ps = ctx.enter_context(tc.psum_pool(name="ps", bufs=1))
+
+        q_raw = sb.tile([P, PACK, Q], F32, name="q_raw")
+        nc.sync.dma_start(out=q_raw[:], in_=query.rearrange("(p j) w -> p j w", j=PACK))
+        g_raw = sb.tile([P, PACK, Q], F32, name="g_raw")
+        nc.sync.dma_start(out=g_raw[:], in_=gout.rearrange("(p j) w -> p j w", j=PACK))
+        keys_v = keys.rearrange("(p j) w -> p j w", j=PACK)
+        n_chunks = T // KEY_CHUNK
+        k_raw = [sb.tile([P, PACK, KEY_CHUNK], F32, name="k_raw%d" % c) for c in range(n_chunks)]
+
+        def load_keys(c):
+            nc.sync.dma_start(out=k_raw[c][:], in_=keys_v[:, :, c * KEY_CHUNK : (c + 1) * KEY_CHUNK])
+
+        load_keys(0)
+        offs_t = sb.tile([P, I // 16], U16, name="offs_t")
+        nc.sync.dma_start(offs_t[:], offs)
+        offs2_t = sb.tile([P, I // 16], U16, name="offs2_t")
+        nc.sync.dma_start(offs2_t[:], offs2)
+        us_cols = sb.tile([P, PACK], F32, name="us_cols")
+        nc.sync.dma_start(out=us_cols[:], in_=us.rearrange("o (p j) -> (o p) j", j=PACK))
+        for c in range(1, n_chunks):
+            load_keys(c)
+        cv_scales = sb.tile([P, T], U8, name="cv_scales", align_bytes=64)
+        for quad in range(4):
+            nc.sync.dma_start(
+                out=cv_scales[32 * quad : 32 * quad + 4, :].bitcast(I32),
+                in_=cvals_scales[0, 4 * quad : 4 * quad + 4, :].bitcast(I32),
+            )
+        cv_words = sb.tile([P, 2 * T], U8, name="cv_words", align_bytes=64)
+        nc.sync.dma_start(out=cv_words[:].bitcast(I32), in_=cvals_words[0].bitcast(I32))
+        corr_v = corr.rearrange("(p j) w -> p j w", j=PACK)
+        planes = []
+        for t in range(PACK):
+            pl = sb.tile([P, U], F32, name="plane%d" % t)
+            nc.sync.dma_start(out=pl[:], in_=corr_v[:, t, :])
+            planes.append(pl)
+        old_t = sb.tile([P, T], F32, name="old_t")
+        nc.sync.dma_start(out=old_t[:], in_=old)
+
+        ident = sb.tile([P, P], F32, name="ident")
+        make_identity(nc, ident[:])
+        s1 = sb.tile([P, T], F32, name="s1")
+        nc.vector.memset(s1[:], 0.0)
+
+        def quantise_rows(raw, label):
+            grouped = sb.tile([P, Q, PACK], BF16, name=label + "_grouped", align_bytes=64)
+            dst, src = weave_views(grouped, raw, 0, Q)
+            nc.vector.tensor_copy(out=dst, in_=src)
+            codes = sb.tile([P, Q], U32, name=label + "_codes", align_bytes=64)
+            scales = sb.tile([P, Q], U8, name=label + "_scales", align_bytes=64)
+            nc.vector.quantize_mx(out=codes[:].bitcast(FP8X4), scales=scales[:], in_=grouped[:].rearrange("p w j -> p (w j)"))
+            return codes, scales
+
+        q_codes, q_scales = quantise_rows(q_raw, "q")
+        g_codes, g_scales = quantise_rows(g_raw, "g")
+
+        a_sb = sb.tile([P, T], F32, name="a_sb")
+        maxes = sb.tile([P, n_chunks], F32, name="maxes")
+        for c in range(n_chunks):
+            grouped = sb.tile([P, KEY_CHUNK, PACK], BF16, name="k_grouped%d" % c, align_bytes=64)
+            dst, src = weave_views(grouped, k_raw[c], 0, KEY_VECTOR)
+            nc.vector.tensor_copy(out=dst, in_=src)
+            dst, src = weave_views(grouped, k_raw[c], KEY_VECTOR, KEY_CHUNK)
+            nc.scalar.activation(out=dst, in_=src, func=ACT.Copy)
+            codes = sb.tile([P, KEY_CHUNK], U32, name="k_codes%d" % c, align_bytes=64)
+            scales = sb.tile([P, KEY_CHUNK], U8, name="k_scales%d" % c, align_bytes=64)
+            nc.vector.quantize_mx(out=codes[:].bitcast(FP8X4), scales=scales[:], in_=grouped[:].rearrange("p w j -> p (w j)"))
+            a_ps = ps.tile([P, KEY_CHUNK], F32, name="a_ps%d" % c, tag="bank%d" % c)
+            nc.tensor.matmul_mx(out=a_ps[:], lhsT=q_codes[:].bitcast(FP8X4), lhsT_scale=q_scales[:],
+                                rhs=codes[:].bitcast(FP8X4), rhs_scale=scales[:], start=True, stop=True)
+            nc.vector.tensor_scalar(out=a_sb[:, c * KEY_CHUNK : (c + 1) * KEY_CHUNK], in0=a_ps[:], scalar1=1.0, scalar2=None,
+                                    op0=ALU.mult, op1=ALU.max, accum_out=maxes[:, c : c + 1])
+        neg_max = sb.tile([P, 1], F32, name="neg_max")
+        nc.vector.tensor_reduce(out=neg_max[:], in_=maxes[:], axis=AXIS.X, op=ALU.max, negate=True)
+        p_sb = sb.tile([P, T], F32, name="p_sb")
+        z = sb.tile([P, 1], F32, name="z")
+        nc.scalar.activation(out=p_sb[:], in_=a_sb[:], func=ACT.Exp, bias=neg_max[:], scale=1.0, accum_out=z[:])
+        a_listed = sb.tile([P, I], F32, name="a_listed")
+        nc.vector.tensor_copy(out=a_listed[:], in_=a_sb[:].indirect(offs_t[:]))
+        px = sb.tile([P, I], F32, name="px")
+        nc.scalar.activation(out=px[:], in_=a_listed[:], func=ACT.Exp, bias=neg_max[:], scale=1.0)
+        rz = sb.tile([P, 1], F32, name="rz")
+        nc.vector.reciprocal(out=rz[:], in_=z[:])
+        rz_gain = sb.tile([P, 1], F32, name="rz_gain")
+        nc.scalar.activation(out=rz_gain[:], in_=rz[:], func=ACT.Copy, scale=GAIN)
+        neg_rz = sb.tile([P, 1], F32, name="neg_rz")
+        nc.scalar.activation(out=neg_rz[:], in_=rz[:], func=ACT.Copy, scale=-1.0)
+
+        us_ps = ps.tile([P, PACK, P], F32, name="us_ps", tag="bank_us")
+        for j in range(PACK):
+            nc.tensor.transpose(us_ps[:, j, :], us_cols[:, j : j + 1].to_broadcast([P, P]), ident[:])
+
+        sums = sb.tile([P, 4], F32, name="sums")
+        pc0 = sb.tile([P, T], F32, name="pc0")
+        for h in range(T // BANK):
+            c0_ps = ps.tile([P, BANK], F32, name="c0_ps%d" % h, tag="bank_c0%d" % h)
+            nc.tensor.matmul_mx(out=c0_ps[:], lhsT=g_codes[:].bitcast(FP8X4), lhsT_scale=g_scales[:],
+                                rhs=cv_words[:, 2 * BANK * h : 2 * BANK * (h + 1)].bitcast(FP4X4),
+                                rhs_scale=cv_scales[:, BANK * h : BANK * (h + 1)], start=True, stop=True)
+            cols = slice(BANK * h, BANK * (h + 1))
+            nc.vector.scalar_tensor_tensor(out=pc0[:, cols], in0=c0_ps[:], scalar=rz_gain[:], in1=p_sb[:, cols],
+                                           op0=ALU.mult, op1=ALU.mult, accum_out=sums[:, h : h + 1])
+        w = sb.tile([P, I], F32, name="w")
+        nc.vector.scalar_tensor_tensor(out=w[:].rearrange("p (n j) -> p n j", j=PACK),
+                                       in0=us_ps[:].rearrange("p j n -> p n j"), scalar=rz_gain[:],
+                                       in1=px[:].rearrange("p (n j) -> p n j", j=PACK), op0=ALU.mult, op1=ALU.mult)
+
+        halves = I // HALF
+        c_grouped = [sb.tile([P, HALF, PACK], BF16, name="c_grouped%d" % h, align_bytes=64) for h in range(halves)]
+        for t in range(PACK):
+            for h in range(halves):
+                nc.vector.tensor_copy(out=c_grouped[h][:, :, t],
+                                      in_=planes[t][:].indirect(offs2_t[:, h * HALF // 16 : (h + 1) * HALF // 16]))
+        c1_ps = []
+        for h in range(halves):
+            codes = sb.tile([P, HALF], U32, name="c_codes%d" % h, align_bytes=64)
+            scales = sb.tile([P, HALF], U8, name="c_scales%d" % h, align_bytes=64)
+            nc.vector.quantize_mx(out=codes[:].bitcast(FP8X4), scales=scales[:], in_=c_grouped[h][:].rearrange("p w j -> p (w j)"))
+            acc = ps.tile([P, HALF], F32, name="c1_ps%d" % h, tag=("bank_c1", "bank_us")[h])
+            nc.tensor.matmul_mx(out=acc[:], lhsT=g_codes[:].bitcast(FP8X4), lhsT_scale=g_scales[:],
+                                rhs=codes[:].bitcast(FP8X4), rhs_scale=scales[:], start=True, stop=True)
+            c1_ps.append(acc)
+        e1 = sb.tile([P, I], F32, name="e1")
+        for h in range(halves):
+            cols = slice(HALF * h, HALF * (h + 1))
+            nc.vector.scalar_tensor_tensor(out=e1[:, cols], in0=c1_ps[h][:], scalar=1.0, in1=w[:, cols],
+                                           op0=ALU.mult, op1=ALU.mult, accum_out=sums[:, 2 + h : 3 + h])
+        nc.vector.tensor_copy(out=s1[:].indirect(offs_t[:]), in_=e1[:])
+
+        scaled_sums = sb.tile([P, 4], F32, name="scaled_sums")
+        dz = sb.tile([P, 1], F32, name="dz")
+        nc.scalar.activation(out=scaled_sums[:], in_=sums[:], func=ACT.Copy, scale=neg_rz[:], accum_out=dz[:])
+        blocks = BANK // P
+        turned = []
+        for h in range(T // BANK):
+            tp = ps.tile([P, BANK], F32, name="turned%d" % h, tag="bank%d" % h)
+            turned.append(tp)
+            for n, term in enumerate((pc0, old_t)):
+                for j in range(blocks):
+                    nc.tensor.matmul(tp[:, j * P : (j + 1) * P], lhsT=term[:, h * BANK + j * P : h * BANK + (j + 1) * P], rhs=ident[:],
+                                     is_transpose=True, start=(n == 0 and j == 0), stop=False)
+        pdz = sb.tile([P, T], F32, name="pdz")
+        for h in range(T // BANK):
+            cols = slice(BANK * h, BANK * (h + 1))
+            nc.scalar.activation(out=pdz[:, cols], in_=p_sb[:, cols], func=ACT.Copy, scale=dz[:])
+            for j in range(blocks):
+                nc.tensor.matmul(turned[h][:, j * P : (j + 1) * P], lhsT=pdz[:, h * BANK + j * P : h * BANK + (j + 1) * P], rhs=ident[:],
+                                 is_transpose=True, start=False, stop=(j == blocks - 1))
+        dense = []
+        for h in range(T // BANK):
+            turned_sb = sb.tile([P, BANK], F32, name="turned_sb%d" % h)
+            nc.scalar.activation(out=turned_sb[:], in_=turned[h][:], func=ACT.Copy)
+            back = ps.tile([P, BANK], F32, name="dense%d" % h, tag="bank%d" % (2 + h))
+            for j in range(blocks):
+                nc.tensor.transpose(back[:, j * P : (j + 1) * P], turned_sb[:, j * P : (j + 1) * P], ident[:])
+            dense.append(back)
+        for s in range(T // STORE):
+            h, lo = divmod(s * STORE, BANK)
+            res = sb.tile([P, STORE], F32, name="res%d" % s)
+            nc.vector.tensor_tensor(out=res[:], in0=dense[h][:, lo : lo + STORE], in1=s1[:, s * STORE : (s + 1) * STORE], op=ALU.add)
+            nc.sync.dma_start(out=out[:, s * STORE : (s + 1) * STORE], in_=res[:])

@@ -16,22 +16,14 @@ FP8X4 = mybir.dt.float8_e4m3fn_x4
 FP4X4 = mybir.dt.float4_e2m1fn_x4
 ALU = mybir.AluOpType
 ACT = mybir.ActivationFunctionType
-AXIS = mybir.AxisListType
 
 P = 128
 PACK = 4
 BANK = 512
-KEY_CHUNK = 256
-KEY_VECTOR = 160
+KEY_CHUNKS = ((0, 256), (256, 512), (512, 768), (768, 1024))
 HALF = 256
 STORE = 256
 GAIN = 1024.0
-
-
-def weave_views(grouped, raw, lo, hi):
-    dst = grouped[:, lo:hi, :].rearrange("p (c i) t -> p c t i", i=4)
-    src = raw[:, :, lo:hi].rearrange("p t (c i) -> p c t i", i=4)
-    return dst, src
 
 
 def tile_attend_bvaluepatch_kernel(tc, query, keys, gout, cvals_words, cvals_scales, corr, us, old, offs, offs2, out):
@@ -42,14 +34,20 @@ def tile_attend_bvaluepatch_kernel(tc, query, keys, gout, cvals_words, cvals_sca
 
         q_raw = sb.tile([P, PACK, Q], F32, name="q_raw")
         nc.sync.dma_start(out=q_raw[:], in_=query.rearrange("(p j) w -> p j w", j=PACK))
-        g_raw = sb.tile([P, PACK, Q], F32, name="g_raw")
-        nc.sync.dma_start(out=g_raw[:], in_=gout.rearrange("(p j) w -> p j w", j=PACK))
         keys_v = keys.rearrange("(p j) w -> p j w", j=PACK)
-        n_chunks = T // KEY_CHUNK
-        k_raw = [sb.tile([P, PACK, KEY_CHUNK], F32, name="k_raw%d" % c) for c in range(n_chunks)]
+        n_chunks = len(KEY_CHUNKS)
+        k_raw = [sb.tile([P, PACK, hi - lo], F32, name="k_raw%d" % lo) for lo, hi in KEY_CHUNKS]
 
         def load_keys(c):
-            nc.sync.dma_start(out=k_raw[c][:], in_=keys_v[:, :, c * KEY_CHUNK : (c + 1) * KEY_CHUNK])
+            nc.sync.dma_start(out=k_raw[c][:], in_=keys_v[:, :, KEY_CHUNKS[c][0] : KEY_CHUNKS[c][1]])
+
+        cv_scales = sb.tile([P, T], U8, name="cv_scales", align_bytes=64)
+
+        def load_scales(quad):
+            nc.sync.dma_start(
+                out=cv_scales[32 * quad : 32 * quad + 4, :].bitcast(I32),
+                in_=cvals_scales[0, 4 * quad : 4 * quad + 4, :].bitcast(I32),
+            )
 
         load_keys(0)
         offs_t = sb.tile([P, I // 16], U16, name="offs_t")
@@ -58,14 +56,13 @@ def tile_attend_bvaluepatch_kernel(tc, query, keys, gout, cvals_words, cvals_sca
         nc.sync.dma_start(offs2_t[:], offs2)
         us_cols = sb.tile([P, PACK], F32, name="us_cols")
         nc.sync.dma_start(out=us_cols[:], in_=us.rearrange("o (p j) -> (o p) j", j=PACK))
+        load_scales(0)
         for c in range(1, n_chunks):
             load_keys(c)
-        cv_scales = sb.tile([P, T], U8, name="cv_scales", align_bytes=64)
-        for quad in range(4):
-            nc.sync.dma_start(
-                out=cv_scales[32 * quad : 32 * quad + 4, :].bitcast(I32),
-                in_=cvals_scales[0, 4 * quad : 4 * quad + 4, :].bitcast(I32),
-            )
+        g_raw = sb.tile([P, PACK, Q], F32, name="g_raw")
+        nc.sync.dma_start(out=g_raw[:], in_=gout.rearrange("(p j) w -> p j w", j=PACK))
+        for quad in range(1, 4):
+            load_scales(quad)
         cv_words = sb.tile([P, 2 * T], U8, name="cv_words", align_bytes=64)
         nc.sync.dma_start(out=cv_words[:].bitcast(I32), in_=cvals_words[0].bitcast(I32))
         corr_v = corr.rearrange("(p j) w -> p j w", j=PACK)
@@ -74,61 +71,80 @@ def tile_attend_bvaluepatch_kernel(tc, query, keys, gout, cvals_words, cvals_sca
             pl = sb.tile([P, U], F32, name="plane%d" % t)
             nc.sync.dma_start(out=pl[:], in_=corr_v[:, t, :])
             planes.append(pl)
-        old_t = sb.tile([P, T], F32, name="old_t")
-        nc.sync.dma_start(out=old_t[:], in_=old)
+        old_t = []
+        for h in range(T // BANK):
+            ot = sb.tile([P, BANK], F32, name="old_t%d" % h)
+            nc.sync.dma_start(out=ot[:], in_=old[:, h * BANK : (h + 1) * BANK])
+            old_t.append(ot)
 
         ident = sb.tile([P, P], F32, name="ident")
         make_identity(nc, ident[:])
         s1 = sb.tile([P, T], F32, name="s1")
-        nc.vector.memset(s1[:], 0.0)
+        nc.gpsimd.memset(s1[:], 0.0)
 
-        def quantise_rows(raw, label):
-            grouped = sb.tile([P, Q, PACK], BF16, name=label + "_grouped", align_bytes=64)
-            dst, src = weave_views(grouped, raw, 0, Q)
-            nc.vector.tensor_copy(out=dst, in_=src)
-            codes = sb.tile([P, Q], U32, name=label + "_codes", align_bytes=64)
-            scales = sb.tile([P, Q], U8, name=label + "_scales", align_bytes=64)
+        def weave(raw, lo, hi, on_vector, label):
+            grouped = sb.tile([P, hi - lo, PACK], BF16, name=label + "_grouped", align_bytes=64)
+            dst = grouped[:].rearrange("p (c i) t -> p c t i", i=4)
+            src = raw[:, :, lo:hi].rearrange("p t (c i) -> p c t i", i=4)
+            if on_vector:
+                nc.vector.tensor_copy(out=dst, in_=src)
+            else:
+                nc.scalar.activation(out=dst, in_=src, func=ACT.Copy)
+            return grouped
+
+        def quantise(grouped, label):
+            width = grouped.shape[1]
+            codes = sb.tile([P, width], U32, name=label + "_codes", align_bytes=64)
+            scales = sb.tile([P, width], U8, name=label + "_scales", align_bytes=64)
             nc.vector.quantize_mx(out=codes[:].bitcast(FP8X4), scales=scales[:], in_=grouped[:].rearrange("p w j -> p (w j)"))
             return codes, scales
 
-        q_codes, q_scales = quantise_rows(q_raw, "q")
-        g_codes, g_scales = quantise_rows(g_raw, "g")
+        q_codes, q_scales = quantise(weave(q_raw, 0, Q, True, "q"), "q")
 
         a_sb = sb.tile([P, T], F32, name="a_sb")
-        maxes = sb.tile([P, n_chunks], F32, name="maxes")
-        for c in range(n_chunks):
-            grouped = sb.tile([P, KEY_CHUNK, PACK], BF16, name="k_grouped%d" % c, align_bytes=64)
-            dst, src = weave_views(grouped, k_raw[c], 0, KEY_VECTOR)
-            nc.vector.tensor_copy(out=dst, in_=src)
-            dst, src = weave_views(grouped, k_raw[c], KEY_VECTOR, KEY_CHUNK)
-            nc.scalar.activation(out=dst, in_=src, func=ACT.Copy)
-            codes = sb.tile([P, KEY_CHUNK], U32, name="k_codes%d" % c, align_bytes=64)
-            scales = sb.tile([P, KEY_CHUNK], U8, name="k_scales%d" % c, align_bytes=64)
-            nc.vector.quantize_mx(out=codes[:].bitcast(FP8X4), scales=scales[:], in_=grouped[:].rearrange("p w j -> p (w j)"))
-            a_ps = ps.tile([P, KEY_CHUNK], F32, name="a_ps%d" % c, tag="bank%d" % c)
+        steps = [(c, 0, hi - lo, c == 1) for c, (lo, hi) in enumerate(KEY_CHUNKS[:-1])]
+        steps = steps + [(n_chunks - 1, 0, P, True), (n_chunks - 1, P, 2 * P, False)]
+        maxes = sb.tile([P, len(steps)], F32, name="maxes")
+        for n, (c, lo, hi, on_vector) in enumerate(steps):
+            codes, scales = quantise(weave(k_raw[c], lo, hi, on_vector, "k%d" % n), "k%d" % n)
+            a_ps = ps.tile([P, hi - lo], F32, name="a_ps%d" % n, tag="bank%d" % (n % 4))
             nc.tensor.matmul_mx(out=a_ps[:], lhsT=q_codes[:].bitcast(FP8X4), lhsT_scale=q_scales[:],
                                 rhs=codes[:].bitcast(FP8X4), rhs_scale=scales[:], start=True, stop=True)
-            nc.vector.tensor_scalar(out=a_sb[:, c * KEY_CHUNK : (c + 1) * KEY_CHUNK], in0=a_ps[:], scalar1=1.0, scalar2=None,
-                                    op0=ALU.mult, op1=ALU.max, accum_out=maxes[:, c : c + 1])
+            first = KEY_CHUNKS[c][0]
+            nc.vector.tensor_scalar(out=a_sb[:, first + lo : first + hi], in0=a_ps[:], scalar1=1.0,
+                                    scalar2=(maxes[:, n - 1 : n] if n > 0 else None),
+                                    op0=ALU.mult, op1=ALU.max, accum_out=maxes[:, n : n + 1])
+        g_codes, g_scales = quantise(weave(g_raw, 0, Q, False, "g"), "g")
         neg_max = sb.tile([P, 1], F32, name="neg_max")
-        nc.vector.tensor_reduce(out=neg_max[:], in_=maxes[:], axis=AXIS.X, op=ALU.max, negate=True)
+        nc.scalar.activation(out=neg_max[:], in_=maxes[:, len(steps) - 1 :], func=ACT.Copy, scale=-1.0)
         p_sb = sb.tile([P, T], F32, name="p_sb")
         z = sb.tile([P, 1], F32, name="z")
         nc.scalar.activation(out=p_sb[:], in_=a_sb[:], func=ACT.Exp, bias=neg_max[:], scale=1.0, accum_out=z[:])
+        z_scaled = sb.tile([P, 1], F32, name="z_scaled")
+        nc.scalar.activation(out=z_scaled[:], in_=z[:], func=ACT.Copy, scale=1.0 / GAIN)
         a_listed = sb.tile([P, I], F32, name="a_listed")
         nc.vector.tensor_copy(out=a_listed[:], in_=a_sb[:].indirect(offs_t[:]))
         px = sb.tile([P, I], F32, name="px")
         nc.scalar.activation(out=px[:], in_=a_listed[:], func=ACT.Exp, bias=neg_max[:], scale=1.0)
-        rz = sb.tile([P, 1], F32, name="rz")
-        nc.vector.reciprocal(out=rz[:], in_=z[:])
         rz_gain = sb.tile([P, 1], F32, name="rz_gain")
-        nc.scalar.activation(out=rz_gain[:], in_=rz[:], func=ACT.Copy, scale=GAIN)
+        nc.vector.reciprocal(out=rz_gain[:], in_=z_scaled[:])
         neg_rz = sb.tile([P, 1], F32, name="neg_rz")
-        nc.scalar.activation(out=neg_rz[:], in_=rz[:], func=ACT.Copy, scale=-1.0)
+        nc.scalar.activation(out=neg_rz[:], in_=rz_gain[:], func=ACT.Copy, scale=-1.0 / GAIN)
 
         us_ps = ps.tile([P, PACK, P], F32, name="us_ps", tag="bank_us")
         for j in range(PACK):
             nc.tensor.transpose(us_ps[:, j, :], us_cols[:, j : j + 1].to_broadcast([P, P]), ident[:])
+
+        halves = I // HALF
+        c_listed = sb.tile([P, halves, PACK, HALF], BF16, name="c_listed")
+
+        def gather_plane(t):
+            if t < PACK - 1:
+                nc.vector.tensor_copy(out=c_listed[:, :, t, :], in_=planes[t][:].indirect(offs2_t[:]))
+            else:
+                for h in range(halves):
+                    nc.vector.tensor_copy(out=c_listed[:, h, t, :],
+                                          in_=planes[t][:].indirect(offs2_t[:, h * HALF // 16 : (h + 1) * HALF // 16]))
 
         sums = sb.tile([P, 4], F32, name="sums")
         pc0 = sb.tile([P, T], F32, name="pc0")
@@ -145,17 +161,12 @@ def tile_attend_bvaluepatch_kernel(tc, query, keys, gout, cvals_words, cvals_sca
                                        in0=us_ps[:].rearrange("p j n -> p n j"), scalar=rz_gain[:],
                                        in1=px[:].rearrange("p (n j) -> p n j", j=PACK), op0=ALU.mult, op1=ALU.mult)
 
-        halves = I // HALF
-        c_grouped = [sb.tile([P, HALF, PACK], BF16, name="c_grouped%d" % h, align_bytes=64) for h in range(halves)]
         for t in range(PACK):
-            for h in range(halves):
-                nc.vector.tensor_copy(out=c_grouped[h][:, :, t],
-                                      in_=planes[t][:].indirect(offs2_t[:, h * HALF // 16 : (h + 1) * HALF // 16]))
+            gather_plane(t)
+        c_grouped = [weave(c_listed[:, h], 0, HALF, h == 1, "c%d" % h) for h in range(halves)]
         c1_ps = []
         for h in range(halves):
-            codes = sb.tile([P, HALF], U32, name="c_codes%d" % h, align_bytes=64)
-            scales = sb.tile([P, HALF], U8, name="c_scales%d" % h, align_bytes=64)
-            nc.vector.quantize_mx(out=codes[:].bitcast(FP8X4), scales=scales[:], in_=c_grouped[h][:].rearrange("p w j -> p (w j)"))
+            codes, scales = quantise(c_grouped[h], "c%d" % h)
             acc = ps.tile([P, HALF], F32, name="c1_ps%d" % h, tag=("bank_c1", "bank_us")[h])
             nc.tensor.matmul_mx(out=acc[:], lhsT=g_codes[:].bitcast(FP8X4), lhsT_scale=g_scales[:],
                                 rhs=codes[:].bitcast(FP8X4), rhs_scale=scales[:], start=True, stop=True)
@@ -170,32 +181,39 @@ def tile_attend_bvaluepatch_kernel(tc, query, keys, gout, cvals_words, cvals_sca
         scaled_sums = sb.tile([P, 4], F32, name="scaled_sums")
         dz = sb.tile([P, 1], F32, name="dz")
         nc.scalar.activation(out=scaled_sums[:], in_=sums[:], func=ACT.Copy, scale=neg_rz[:], accum_out=dz[:])
-        blocks = BANK // P
+        pieces = T // STORE
+        blocks = STORE // P
         turned = []
-        for h in range(T // BANK):
-            tp = ps.tile([P, BANK], F32, name="turned%d" % h, tag="bank%d" % h)
+        for n in range(pieces):
+            tp = ps.tile([P, STORE], F32, name="turned%d" % n, tag="bank%d" % n)
             turned.append(tp)
-            for n, term in enumerate((pc0, old_t)):
+            h, lo = divmod(n * STORE, BANK)
+            for m, term in enumerate((pc0[:, n * STORE : (n + 1) * STORE], old_t[h][:, lo : lo + STORE])):
                 for j in range(blocks):
-                    nc.tensor.matmul(tp[:, j * P : (j + 1) * P], lhsT=term[:, h * BANK + j * P : h * BANK + (j + 1) * P], rhs=ident[:],
-                                     is_transpose=True, start=(n == 0 and j == 0), stop=False)
-        pdz = sb.tile([P, T], F32, name="pdz")
-        for h in range(T // BANK):
-            cols = slice(BANK * h, BANK * (h + 1))
-            nc.scalar.activation(out=pdz[:, cols], in_=p_sb[:, cols], func=ACT.Copy, scale=dz[:])
-            for j in range(blocks):
-                nc.tensor.matmul(turned[h][:, j * P : (j + 1) * P], lhsT=pdz[:, h * BANK + j * P : h * BANK + (j + 1) * P], rhs=ident[:],
-                                 is_transpose=True, start=False, stop=(j == blocks - 1))
+                    nc.tensor.matmul(tp[:, j * P : (j + 1) * P], lhsT=term[:, j * P : (j + 1) * P], rhs=ident[:],
+                                     is_transpose=True, start=(m == 0 and j == 0), stop=False)
         dense = []
-        for h in range(T // BANK):
-            turned_sb = sb.tile([P, BANK], F32, name="turned_sb%d" % h)
-            nc.scalar.activation(out=turned_sb[:], in_=turned[h][:], func=ACT.Copy)
-            back = ps.tile([P, BANK], F32, name="dense%d" % h, tag="bank%d" % (2 + h))
+
+        def scale_piece(n):
+            pdz = sb.tile([P, STORE], F32, name="pdz%d" % n)
+            nc.scalar.activation(out=pdz[:], in_=p_sb[:, n * STORE : (n + 1) * STORE], func=ACT.Copy, scale=dz[:])
+            for j in range(blocks):
+                nc.tensor.matmul(turned[n][:, j * P : (j + 1) * P], lhsT=pdz[:, j * P : (j + 1) * P], rhs=ident[:],
+                                 is_transpose=True, start=False, stop=(j == blocks - 1))
+
+        def turn_back(n):
+            turned_sb = sb.tile([P, STORE], F32, name="turned_sb%d" % n)
+            nc.scalar.activation(out=turned_sb[:], in_=turned[n][:], func=ACT.Copy)
+            back = ps.tile([P, STORE], F32, name="dense%d" % n, tag=("bank_c00", "bank_c01", "bank_c1", "bank_us")[n])
             for j in range(blocks):
                 nc.tensor.transpose(back[:, j * P : (j + 1) * P], turned_sb[:, j * P : (j + 1) * P], ident[:])
             dense.append(back)
-        for s in range(T // STORE):
-            h, lo = divmod(s * STORE, BANK)
-            res = sb.tile([P, STORE], F32, name="res%d" % s)
-            nc.vector.tensor_tensor(out=res[:], in0=dense[h][:, lo : lo + STORE], in1=s1[:, s * STORE : (s + 1) * STORE], op=ALU.add)
-            nc.sync.dma_start(out=out[:, s * STORE : (s + 1) * STORE], in_=res[:])
+
+        for n in range(pieces):
+            scale_piece(n)
+        for n in range(pieces):
+            turn_back(n)
+        for n in range(pieces):
+            res = sb.tile([P, STORE], F32, name="res%d" % n)
+            nc.vector.tensor_tensor(out=res[:], in0=dense[n][:], in1=s1[:, n * STORE : (n + 1) * STORE], op=ALU.add)
+            nc.sync.dma_start(out=out[:, n * STORE : (n + 1) * STORE], in_=res[:])

@@ -21,6 +21,7 @@ P = 128
 PACK = 4
 BANK = 512
 KEY_CHUNKS = ((0, 256), (256, 512), (512, 768), (768, 1024))
+KEY_VECTOR_COLS = (0, 256, 0, 128)
 HALF = 256
 STORE = 256
 GAIN = 1024.0
@@ -68,7 +69,7 @@ def tile_attend_bvaluepatch_kernel(tc, query, keys, gout, cvals_words, cvals_sca
         corr_v = corr.rearrange("(p j) w -> p j w", j=PACK)
         planes = []
         for t in range(PACK):
-            pl = sb.tile([P, U], F32, name="plane%d" % t)
+            pl = sb.tile([P, U], F32, name="plane%d" % t, tag="plane%d" % t)
             nc.sync.dma_start(out=pl[:], in_=corr_v[:, t, :])
             planes.append(pl)
         old_t = []
@@ -82,14 +83,17 @@ def tile_attend_bvaluepatch_kernel(tc, query, keys, gout, cvals_words, cvals_sca
         s1 = sb.tile([P, T], F32, name="s1")
         nc.gpsimd.memset(s1[:], 0.0)
 
-        def weave(raw, lo, hi, on_vector, label):
-            grouped = sb.tile([P, hi - lo, PACK], BF16, name=label + "_grouped", align_bytes=64)
-            dst = grouped[:].rearrange("p (c i) t -> p c t i", i=4)
-            src = raw[:, :, lo:hi].rearrange("p t (c i) -> p c t i", i=4)
-            if on_vector:
-                nc.vector.tensor_copy(out=dst, in_=src)
-            else:
-                nc.scalar.activation(out=dst, in_=src, func=ACT.Copy)
+        def weave(raw, vector_cols, label, tag):
+            width = raw.shape[2]
+            grouped = sb.tile([P, width, PACK], BF16, name=label + "_grouped", tag=tag, align_bytes=64)
+            for lo, hi, on_vector in ((0, vector_cols, True), (vector_cols, width, False)):
+                if hi > lo:
+                    dst = grouped[:, lo:hi, :].rearrange("p (c i) t -> p c t i", i=4)
+                    src = raw[:, :, lo:hi].rearrange("p t (c i) -> p c t i", i=4)
+                    if on_vector:
+                        nc.vector.tensor_copy(out=dst, in_=src)
+                    else:
+                        nc.scalar.activation(out=dst, in_=src, func=ACT.Copy)
             return grouped
 
         def quantise(grouped, label):
@@ -99,24 +103,34 @@ def tile_attend_bvaluepatch_kernel(tc, query, keys, gout, cvals_words, cvals_sca
             nc.vector.quantize_mx(out=codes[:].bitcast(FP8X4), scales=scales[:], in_=grouped[:].rearrange("p w j -> p (w j)"))
             return codes, scales
 
-        q_codes, q_scales = quantise(weave(q_raw, 0, Q, True, "q"), "q")
+        q_codes, q_scales = quantise(weave(q_raw, Q, "q", "grouped_q"), "q")
 
         a_sb = sb.tile([P, T], F32, name="a_sb")
-        steps = [(c, 0, hi - lo, c == 1) for c, (lo, hi) in enumerate(KEY_CHUNKS[:-1])]
-        steps = steps + [(n_chunks - 1, 0, P, True), (n_chunks - 1, P, 2 * P, False)]
-        maxes = sb.tile([P, len(steps)], F32, name="maxes")
-        for n, (c, lo, hi, on_vector) in enumerate(steps):
-            codes, scales = quantise(weave(k_raw[c], lo, hi, on_vector, "k%d" % n), "k%d" % n)
-            a_ps = ps.tile([P, hi - lo], F32, name="a_ps%d" % n, tag="bank%d" % (n % 4))
+        score_banks = []
+        running_max = [None]
+
+        def score_chunk(c):
+            codes, scales = quantise(weave(k_raw[c], KEY_VECTOR_COLS[c], "k%d" % c, "grouped%d" % c), "k%d" % c)
+            a_ps = ps.tile([P, codes.shape[1]], F32, name="a_ps%d" % c, tag="bank%d" % c)
             nc.tensor.matmul_mx(out=a_ps[:], lhsT=q_codes[:].bitcast(FP8X4), lhsT_scale=q_scales[:],
                                 rhs=codes[:].bitcast(FP8X4), rhs_scale=scales[:], start=True, stop=True)
-            first = KEY_CHUNKS[c][0]
-            nc.vector.tensor_scalar(out=a_sb[:, first + lo : first + hi], in0=a_ps[:], scalar1=1.0,
-                                    scalar2=(maxes[:, n - 1 : n] if n > 0 else None),
-                                    op0=ALU.mult, op1=ALU.max, accum_out=maxes[:, n : n + 1])
-        g_codes, g_scales = quantise(weave(g_raw, 0, Q, False, "g"), "g")
+            score_banks.append(a_ps)
+
+        def drain_chunk(c):
+            lo, hi = KEY_CHUNKS[c]
+            new_max = sb.tile([P, 1], F32, name="max%d" % c, tag="grouped%d" % (c + 1), align_bytes=64)
+            nc.vector.tensor_scalar(out=a_sb[:, lo:hi], in0=score_banks[c][:], scalar1=1.0, scalar2=running_max[c],
+                                    op0=ALU.mult, op1=ALU.max, accum_out=new_max[:])
+            running_max.append(new_max[:])
+
+        for c in range(n_chunks + 1):
+            if c < n_chunks:
+                score_chunk(c)
+            if c > 0:
+                drain_chunk(c - 1)
+        g_codes, g_scales = quantise(weave(g_raw, 0, "g", "grouped_q"), "g")
         neg_max = sb.tile([P, 1], F32, name="neg_max")
-        nc.scalar.activation(out=neg_max[:], in_=maxes[:, len(steps) - 1 :], func=ACT.Copy, scale=-1.0)
+        nc.scalar.activation(out=neg_max[:], in_=running_max[n_chunks], func=ACT.Copy, scale=-1.0)
         p_sb = sb.tile([P, T], F32, name="p_sb")
         z = sb.tile([P, 1], F32, name="z")
         nc.scalar.activation(out=p_sb[:], in_=a_sb[:], func=ACT.Exp, bias=neg_max[:], scale=1.0, accum_out=z[:])
@@ -124,9 +138,12 @@ def tile_attend_bvaluepatch_kernel(tc, query, keys, gout, cvals_words, cvals_sca
         nc.scalar.activation(out=z_scaled[:], in_=z[:], func=ACT.Copy, scale=1.0 / GAIN)
         a_listed = sb.tile([P, I], F32, name="a_listed")
         nc.vector.tensor_copy(out=a_listed[:], in_=a_sb[:].indirect(offs_t[:]))
-        px = sb.tile([P, I], F32, name="px")
+        px = sb.tile([P, I], F32, name="px", tag="px")
         nc.scalar.activation(out=px[:], in_=a_listed[:], func=ACT.Exp, bias=neg_max[:], scale=1.0)
-        rz_gain = sb.tile([P, 1], F32, name="rz_gain")
+        halves = I // HALF
+        low = sb.tile([P, halves, 2, HALF], BF16, name="listed_low")
+        nc.vector.tensor_copy(out=low[:, :, 0, :], in_=planes[0][:].indirect(offs2_t[:]))
+        rz_gain = sb.tile([P, 1], F32, name="rz_gain", tag="plane0")
         nc.vector.reciprocal(out=rz_gain[:], in_=z_scaled[:])
         neg_rz = sb.tile([P, 1], F32, name="neg_rz")
         nc.scalar.activation(out=neg_rz[:], in_=rz_gain[:], func=ACT.Copy, scale=-1.0 / GAIN)
@@ -134,17 +151,6 @@ def tile_attend_bvaluepatch_kernel(tc, query, keys, gout, cvals_words, cvals_sca
         us_ps = ps.tile([P, PACK, P], F32, name="us_ps", tag="bank_us")
         for j in range(PACK):
             nc.tensor.transpose(us_ps[:, j, :], us_cols[:, j : j + 1].to_broadcast([P, P]), ident[:])
-
-        halves = I // HALF
-        c_listed = sb.tile([P, halves, PACK, HALF], BF16, name="c_listed")
-
-        def gather_plane(t):
-            if t < PACK - 1:
-                nc.vector.tensor_copy(out=c_listed[:, :, t, :], in_=planes[t][:].indirect(offs2_t[:]))
-            else:
-                for h in range(halves):
-                    nc.vector.tensor_copy(out=c_listed[:, h, t, :],
-                                          in_=planes[t][:].indirect(offs2_t[:, h * HALF // 16 : (h + 1) * HALF // 16]))
 
         sums = sb.tile([P, 4], F32, name="sums")
         pc0 = sb.tile([P, T], F32, name="pc0")
@@ -161,9 +167,26 @@ def tile_attend_bvaluepatch_kernel(tc, query, keys, gout, cvals_words, cvals_sca
                                        in0=us_ps[:].rearrange("p j n -> p n j"), scalar=rz_gain[:],
                                        in1=px[:].rearrange("p (n j) -> p n j", j=PACK), op0=ALU.mult, op1=ALU.mult)
 
-        for t in range(PACK):
-            gather_plane(t)
-        c_grouped = [weave(c_listed[:, h], 0, HALF, h == 1, "c%d" % h) for h in range(halves)]
+        c_grouped = [sb.tile([P, HALF, PACK], BF16, name="c_grouped%d" % h, align_bytes=64) for h in range(halves)]
+
+        def weave_pair(listed, pair, h, on_vector):
+            dst = c_grouped[h][:, :, 2 * pair : 2 * pair + 2].rearrange("p (c i) t -> p c t i", i=4)
+            src = listed[:, h].rearrange("p t (c i) -> p c t i", i=4)
+            if on_vector:
+                nc.vector.tensor_copy(out=dst, in_=src)
+            else:
+                nc.scalar.activation(out=dst, in_=src, func=ACT.Copy)
+
+        nc.vector.tensor_copy(out=low[:, :, 1, :], in_=planes[1][:].indirect(offs2_t[:]))
+        for h in range(halves):
+            weave_pair(low, 0, h, False)
+        high = sb.tile([P, halves, 2, HALF], BF16, name="listed_high", tag="px")
+        nc.vector.tensor_copy(out=high[:, :, 0, :], in_=planes[2][:].indirect(offs2_t[:]))
+        for h in range(halves):
+            nc.vector.tensor_copy(out=high[:, h, 1, :],
+                                  in_=planes[3][:].indirect(offs2_t[:, h * HALF // 16 : (h + 1) * HALF // 16]))
+        for h in range(halves):
+            weave_pair(high, 1, h, h == 1)
         c1_ps = []
         for h in range(halves):
             codes, scales = quantise(c_grouped[h], "c%d" % h)

@@ -33,6 +33,8 @@ def tile_attend_bvaluepatch_kernel(tc, query, keys, gout, cvals_words, cvals_sca
         sb = ctx.enter_context(tc.tile_pool(name="sb", bufs=1))
         ps = ctx.enter_context(tc.psum_pool(name="ps", bufs=1))
 
+        us_cols = sb.tile([P, PACK], F32, name="us_cols")
+        nc.sync.dma_start(out=us_cols[:], in_=us.rearrange("o (p j) -> (o p) j", j=PACK))
         q_raw = sb.tile([P, PACK, Q], F32, name="q_raw")
         nc.sync.dma_start(out=q_raw[:], in_=query.rearrange("(p j) w -> p j w", j=PACK))
         keys_v = keys.rearrange("(p j) w -> p j w", j=PACK)
@@ -55,8 +57,6 @@ def tile_attend_bvaluepatch_kernel(tc, query, keys, gout, cvals_words, cvals_sca
         nc.sync.dma_start(offs_t[:], offs)
         offs2_t = sb.tile([P, I // 16], U16, name="offs2_t")
         nc.sync.dma_start(offs2_t[:], offs2)
-        us_cols = sb.tile([P, PACK], F32, name="us_cols")
-        nc.sync.dma_start(out=us_cols[:], in_=us.rearrange("o (p j) -> (o p) j", j=PACK))
         load_scales(0)
         for c in range(1, n_chunks):
             load_keys(c)
@@ -82,6 +82,12 @@ def tile_attend_bvaluepatch_kernel(tc, query, keys, gout, cvals_words, cvals_sca
         make_identity(nc, ident[:])
         s1 = sb.tile([P, T], F32, name="s1")
         nc.gpsimd.memset(s1[:], 0.0)
+
+        us_ps = ps.tile([P, PACK, P], F32, name="us_ps", tag="bank_us")
+        for j in range(PACK):
+            nc.tensor.transpose(us_ps[:, j, :], us_cols[:, j : j + 1].to_broadcast([P, P]), ident[:])
+        us_rows = sb.tile([P, P, PACK], F32, name="us_rows")
+        nc.scalar.activation(out=us_rows[:], in_=us_ps[:].rearrange("p j n -> p n j"), func=ACT.Copy)
 
         def weave(raw, vector_cols, label, tag):
             width = raw.shape[2]
@@ -148,10 +154,6 @@ def tile_attend_bvaluepatch_kernel(tc, query, keys, gout, cvals_words, cvals_sca
         neg_rz = sb.tile([P, 1], F32, name="neg_rz")
         nc.scalar.activation(out=neg_rz[:], in_=rz_gain[:], func=ACT.Copy, scale=-1.0 / GAIN)
 
-        us_ps = ps.tile([P, PACK, P], F32, name="us_ps", tag="bank_us")
-        for j in range(PACK):
-            nc.tensor.transpose(us_ps[:, j, :], us_cols[:, j : j + 1].to_broadcast([P, P]), ident[:])
-
         sums = sb.tile([P, 4], F32, name="sums")
         pc0 = sb.tile([P, T], F32, name="pc0")
         for h in range(T // BANK):
@@ -163,15 +165,13 @@ def tile_attend_bvaluepatch_kernel(tc, query, keys, gout, cvals_words, cvals_sca
             nc.vector.scalar_tensor_tensor(out=pc0[:, cols], in0=c0_ps[:], scalar=rz_gain[:], in1=p_sb[:, cols],
                                            op0=ALU.mult, op1=ALU.mult, accum_out=sums[:, h : h + 1])
         w = sb.tile([P, I], F32, name="w")
-        nc.vector.scalar_tensor_tensor(out=w[:].rearrange("p (n j) -> p n j", j=PACK),
-                                       in0=us_ps[:].rearrange("p j n -> p n j"), scalar=rz_gain[:],
-                                       in1=px[:].rearrange("p (n j) -> p n j", j=PACK), op0=ALU.mult, op1=ALU.mult)
+        nc.gpsimd.tensor_tensor(out=w[:], in0=px[:], in1=us_rows[:].rearrange("p n j -> p (n j)"), op=ALU.mult)
 
         c_grouped = [sb.tile([P, HALF, PACK], BF16, name="c_grouped%d" % h, align_bytes=64) for h in range(halves)]
 
         def weave_pair(listed, pair, h, on_vector):
-            dst = c_grouped[h][:, :, 2 * pair : 2 * pair + 2].rearrange("p (c i) t -> p c t i", i=4)
-            src = listed[:, h].rearrange("p t (c i) -> p c t i", i=4)
+            dst = c_grouped[h][:, :, 2 * pair : 2 * pair + 2]
+            src = listed[:, h].rearrange("p t w -> p w t")
             if on_vector:
                 nc.vector.tensor_copy(out=dst, in_=src)
             else:
@@ -197,7 +197,7 @@ def tile_attend_bvaluepatch_kernel(tc, query, keys, gout, cvals_words, cvals_sca
         e1 = sb.tile([P, I], F32, name="e1")
         for h in range(halves):
             cols = slice(HALF * h, HALF * (h + 1))
-            nc.vector.scalar_tensor_tensor(out=e1[:, cols], in0=c1_ps[h][:], scalar=1.0, in1=w[:, cols],
+            nc.vector.scalar_tensor_tensor(out=e1[:, cols], in0=c1_ps[h][:], scalar=rz_gain[:], in1=w[:, cols],
                                            op0=ALU.mult, op1=ALU.mult, accum_out=sums[:, 2 + h : 3 + h])
         nc.vector.tensor_copy(out=s1[:].indirect(offs_t[:]), in_=e1[:])
 

from contextlib import ExitStack

import concourse.mybir as mybir
from concourse.masks import make_identity

D, E, T, I, U, Q = 512, 512, 1024, 512, 2048, 128
FLOPS = 2 * Q * (D * T + E * T + E * I)

F32 = mybir.dt.float32
BF16 = mybir.dt.bfloat16
I32 = mybir.dt.int32
U32 = mybir.dt.uint32
U16 = mybir.dt.uint16
U8 = mybir.dt.uint8
FP8X4 = mybir.dt.float8_e4m3fn_x4
FP4X4 = mybir.dt.float4_e2m1fn_x4
ALU = mybir.AluOpType
ACT = mybir.ActivationFunctionType

P = 128
PACK = 4
BANK = 512
KEY_CHUNKS = ((0, 256), (256, 512), (512, 768), (768, 1024))
KEY_VECTOR_COLS = (0, 256, 0, 128)
HALF = 256
STORE = 256
GAIN = 1024.0


def tile_attend_bvaluepatch_kernel(tc, query, keys, gout, cvals_words, cvals_scales, corr, us, old, offs, offs2, out):
    nc = tc.nc
    with ExitStack() as ctx:
        sb = ctx.enter_context(tc.tile_pool(name="sb", bufs=1))
        ps = ctx.enter_context(tc.psum_pool(name="ps", bufs=1))

        us_cols = sb.tile([P, PACK], F32, name="us_cols")
        nc.sync.dma_start(out=us_cols[:], in_=us.rearrange("o (p j) -> (o p) j", j=PACK))
        q_raw = sb.tile([P, PACK, Q], F32, name="q_raw")
        nc.sync.dma_start(out=q_raw[:], in_=query.rearrange("(p j) w -> p j w", j=PACK))
        keys_v = keys.rearrange("(p j) w -> p j w", j=PACK)
        n_chunks = len(KEY_CHUNKS)
        k_raw = [sb.tile([P, PACK, hi - lo], F32, name="k_raw%d" % lo) for lo, hi in KEY_CHUNKS]

        def load_keys(c):
            nc.sync.dma_start(out=k_raw[c][:], in_=keys_v[:, :, KEY_CHUNKS[c][0] : KEY_CHUNKS[c][1]])

        cv_scales = sb.tile([P, T], U8, name="cv_scales", align_bytes=64)

        def load_scales(quad):
            nc.sync.dma_start(
                out=cv_scales[32 * quad : 32 * quad + 4, :].bitcast(I32),
                in_=cvals_scales[0, 4 * quad : 4 * quad + 4, :].bitcast(I32),
            )

        load_keys(0)
        offs_t = sb.tile([P, I // 16], U16, name="offs_t")
        nc.sync.dma_start(offs_t[:], offs)
        offs2_t = sb.tile([P, I // 16], U16, name="offs2_t")
        nc.sync.dma_start(offs2_t[:], offs2)
        load_scales(0)
        for c in range(1, n_chunks):
            load_keys(c)
        g_raw = sb.tile([P, PACK, Q], F32, name="g_raw")
        nc.sync.dma_start(out=g_raw[:], in_=gout.rearrange("(p j) w -> p j w", j=PACK))
        for quad in range(1, 4):
            load_scales(quad)
        cv_words = sb.tile([P, 2 * T], U8, name="cv_words", align_bytes=64)
        nc.sync.dma_start(out=cv_words[:].bitcast(I32), in_=cvals_words[0].bitcast(I32))
        corr_v = corr.rearrange("(p j) w -> p j w", j=PACK)
        planes = []
        for t in range(PACK):
            pl = sb.tile([P, U], F32, name="plane%d" % t, tag="plane%d" % t)
            nc.sync.dma_start(out=pl[:], in_=corr_v[:, t, :])
            planes.append(pl)
        old_t = []
        for h in range(T // BANK):
            ot = sb.tile([P, BANK], F32, name="old_t%d" % h)
            nc.sync.dma_start(out=ot[:], in_=old[:, h * BANK : (h + 1) * BANK])
            old_t.append(ot)

        ident = sb.tile([P, P], F32, name="ident")
        make_identity(nc, ident[:])
        s1 = sb.tile([P, T], F32, name="s1")
        nc.gpsimd.memset(s1[:], 0.0)

        us_ps = ps.tile([P, PACK, P], F32, name="us_ps", tag="bank_us")
        for j in range(PACK):
            nc.tensor.transpose(us_ps[:, j, :], us_cols[:, j : j + 1].to_broadcast([P, P]), ident[:])
        us_rows = sb.tile([P, P, PACK], F32, name="us_rows")
        nc.scalar.activation(out=us_rows[:], in_=us_ps[:].rearrange("p j n -> p n j"), func=ACT.Copy)

        def weave(raw, vector_cols, label, tag):
            width = raw.shape[2]
            grouped = sb.tile([P, width, PACK], BF16, name=label + "_grouped", tag=tag, align_bytes=64)
            for lo, hi, on_vector in ((0, vector_cols, True), (vector_cols, width, False)):
                if hi > lo:
                    dst = grouped[:, lo:hi, :].rearrange("p (c i) t -> p c t i", i=4)
                    src = raw[:, :, lo:hi].rearrange("p t (c i) -> p c t i", i=4)
                    if on_vector:
                        nc.vector.tensor_copy(out=dst, in_=src)
                    else:
                        nc.scalar.activation(out=dst, in_=src, func=ACT.Copy)
            return grouped

        def quantise(grouped, label):
            width = grouped.shape[1]
            codes = sb.tile([P, width], U32, name=label + "_codes", align_bytes=64)
            scales = sb.tile([P, width], U8, name=label + "_scales", align_bytes=64)
            nc.vector.quantize_mx(out=codes[:].bitcast(FP8X4), scales=scales[:], in_=grouped[:].rearrange("p w j -> p (w j)"))
            return codes, scales

        q_codes, q_scales = quantise(weave(q_raw, Q, "q", "grouped_q"), "q")

        a_sb = sb.tile([P, T], F32, name="a_sb")
        score_banks = []
        running_max = [None]

        def score_chunk(c):
            codes, scales = quantise(weave(k_raw[c], KEY_VECTOR_COLS[c], "k%d" % c, "grouped%d" % c), "k%d" % c)
            a_ps = ps.tile([P, codes.shape[1]], F32, name="a_ps%d" % c, tag="bank%d" % c)
            nc.tensor.matmul_mx(out=a_ps[:], lhsT=q_codes[:].bitcast(FP8X4), lhsT_scale=q_scales[:],
                                rhs=codes[:].bitcast(FP8X4), rhs_scale=scales[:], start=True, stop=True)
            score_banks.append(a_ps)

        def drain_chunk(c):
            lo, hi = KEY_CHUNKS[c]
            new_max = sb.tile([P, 1], F32, name="max%d" % c, tag="grouped%d" % (c + 1), align_bytes=64)
            nc.vector.tensor_scalar(out=a_sb[:, lo:hi], in0=score_banks[c][:], scalar1=1.0, scalar2=running_max[c],
                                    op0=ALU.mult, op1=ALU.max, accum_out=new_max[:])
            running_max.append(new_max[:])

        for c in range(n_chunks + 1):
            if c < n_chunks:
                score_chunk(c)
            if c > 0:
                drain_chunk(c - 1)
        g_codes, g_scales = quantise(weave(g_raw, 0, "g", "grouped_q"), "g")
        neg_max = sb.tile([P, 1], F32, name="neg_max")
        nc.scalar.activation(out=neg_max[:], in_=running_max[n_chunks], func=ACT.Copy, scale=-1.0)
        p_sb = sb.tile([P, T], F32, name="p_sb")
        z = sb.tile([P, 1], F32, name="z")
        nc.scalar.activation(out=p_sb[:], in_=a_sb[:], func=ACT.Exp, bias=neg_max[:], scale=1.0, accum_out=z[:])
        z_scaled = sb.tile([P, 1], F32, name="z_scaled")
        nc.scalar.activation(out=z_scaled[:], in_=z[:], func=ACT.Copy, scale=1.0 / GAIN)
        a_listed = sb.tile([P, I], F32, name="a_listed")
        nc.vector.tensor_copy(out=a_listed[:], in_=a_sb[:].indirect(offs_t[:]))
        px = sb.tile([P, I], F32, name="px", tag="px")
        nc.scalar.activation(out=px[:], in_=a_listed[:], func=ACT.Exp, bias=neg_max[:], scale=1.0)
        halves = I // HALF
        low = sb.tile([P, halves, 2, HALF], BF16, name="listed_low")
        nc.vector.tensor_copy(out=low[:, :, 0, :], in_=planes[0][:].indirect(offs2_t[:]))
        rz_gain = sb.tile([P, 1], F32, name="rz_gain", tag="plane0")
        nc.vector.reciprocal(out=rz_gain[:], in_=z_scaled[:])
        neg_rz = sb.tile([P, 1], F32, name="neg_rz")
        nc.scalar.activation(out=neg_rz[:], in_=rz_gain[:], func=ACT.Copy, scale=-1.0 / GAIN)

        sums = sb.tile([P, 4], F32, name="sums")
        pc0 = sb.tile([P, T], F32, name="pc0")
        for h in range(T // BANK):
            c0_ps = ps.tile([P, BANK], F32, name="c0_ps%d" % h, tag="bank_c0%d" % h)
            nc.tensor.matmul_mx(out=c0_ps[:], lhsT=g_codes[:].bitcast(FP8X4), lhsT_scale=g_scales[:],
                                rhs=cv_words[:, 2 * BANK * h : 2 * BANK * (h + 1)].bitcast(FP4X4),
                                rhs_scale=cv_scales[:, BANK * h : BANK * (h + 1)], start=True, stop=True)
            cols = slice(BANK * h, BANK * (h + 1))
            nc.vector.scalar_tensor_tensor(out=pc0[:, cols], in0=c0_ps[:], scalar=rz_gain[:], in1=p_sb[:, cols],
                                           op0=ALU.mult, op1=ALU.mult, accum_out=sums[:, h : h + 1])
        w = sb.tile([P, I], F32, name="w")
        nc.gpsimd.tensor_tensor(out=w[:], in0=px[:], in1=us_rows[:].rearrange("p n j -> p (n j)"), op=ALU.mult)

        c_grouped = [sb.tile([P, HALF, PACK], BF16, name="c_grouped%d" % h, align_bytes=64) for h in range(halves)]

        def weave_pair(listed, pair, h, on_vector):
            dst = c_grouped[h][:, :, 2 * pair : 2 * pair + 2]
            src = listed[:, h].rearrange("p t w -> p w t")
            if on_vector:
                nc.vector.tensor_copy(out=dst, in_=src)
            else:
                nc.scalar.activation(out=dst, in_=src, func=ACT.Copy)

        nc.vector.tensor_copy(out=low[:, :, 1, :], in_=planes[1][:].indirect(offs2_t[:]))
        for h in range(halves):
            weave_pair(low, 0, h, False)
        high = sb.tile([P, halves, 2, HALF], BF16, name="listed_high", tag="px")
        nc.vector.tensor_copy(out=high[:, :, 0, :], in_=planes[2][:].indirect(offs2_t[:]))
        for h in range(halves):
            nc.vector.tensor_copy(out=high[:, h, 1, :],
                                  in_=planes[3][:].indirect(offs2_t[:, h * HALF // 16 : (h + 1) * HALF // 16]))
        for h in range(halves):
            weave_pair(high, 1, h, h == 1)
        c1_ps = []
        for h in range(halves):
            codes, scales = quantise(c_grouped[h], "c%d" % h)
            acc = ps.tile([P, HALF], F32, name="c1_ps%d" % h, tag=("bank_c1", "bank_us")[h])
            nc.tensor.matmul_mx(out=acc[:], lhsT=g_codes[:].bitcast(FP8X4), lhsT_scale=g_scales[:],
                                rhs=codes[:].bitcast(FP8X4), rhs_scale=scales[:], start=True, stop=True)
            c1_ps.append(acc)
        e1 = sb.tile([P, I], F32, name="e1")
        for h in range(halves):
            cols = slice(HALF * h, HALF * (h + 1))
            nc.vector.scalar_tensor_tensor(out=e1[:, cols], in0=c1_ps[h][:], scalar=rz_gain[:], in1=w[:, cols],
                                           op0=ALU.mult, op1=ALU.mult, accum_out=sums[:, 2 + h : 3 + h])
        nc.vector.tensor_copy(out=s1[:].indirect(offs_t[:]), in_=e1[:])

        scaled_sums = sb.tile([P, 4], F32, name="scaled_sums")
        dz = sb.tile([P, 1], F32, name="dz")
        nc.scalar.activation(out=scaled_sums[:], in_=sums[:], func=ACT.Copy, scale=neg_rz[:], accum_out=dz[:])
        pieces = T // STORE
        blocks = STORE // P
        turned = []
        for n in range(pieces):
            tp = ps.tile([P, STORE], F32, name="turned%d" % n, tag="bank%d" % n)
            turned.append(tp)
            h, lo = divmod(n * STORE, BANK)
            for m, term in enumerate((pc0[:, n * STORE : (n + 1) * STORE], old_t[h][:, lo : lo + STORE])):
                for j in range(blocks):
                    nc.tensor.matmul(tp[:, j * P : (j + 1) * P], lhsT=term[:, j * P : (j + 1) * P], rhs=ident[:],
                                     is_transpose=True, start=(m == 0 and j == 0), stop=False)
        dense = []

        def scale_piece(n):
            pdz = sb.tile([P, STORE], F32, name="pdz%d" % n)
            nc.scalar.activation(out=pdz[:], in_=p_sb[:, n * STORE : (n + 1) * STORE], func=ACT.Copy, scale=dz[:])
            for j in range(blocks):
                nc.tensor.matmul(turned[n][:, j * P : (j + 1) * P], lhsT=pdz[:, j * P : (j + 1) * P], rhs=ident[:],
                                 is_transpose=True, start=False, stop=(j == blocks - 1))

        def turn_back(n):
            turned_sb = sb.tile([P, STORE], F32, name="turned_sb%d" % n)
            nc.scalar.activation(out=turned_sb[:], in_=turned[n][:], func=ACT.Copy)
            back = ps.tile([P, STORE], F32, name="dense%d" % n, tag=("bank_c00", "bank_c01", "bank_c1", "bank_us")[n])
            for j in range(blocks):
                nc.tensor.transpose(back[:, j * P : (j + 1) * P], turned_sb[:, j * P : (j + 1) * P], ident[:])
            dense.append(back)

        for n in range(pieces):
            scale_piece(n)
        for n in range(pieces):
            turn_back(n)
        for n in range(pieces):
            res = sb.tile([P, STORE], F32, name="res%d" % n)
            nc.vector.tensor_tensor(out=res[:], in0=dense[n][:], in1=s1[:, n * STORE : (n + 1) * STORE], op=ALU.add)
            nc.sync.dma_start(out=out[:, n * STORE : (n + 1) * STORE], in_=res[:])
